import numpy as np, ml_dtypes
CORES = [25,29,65,69,153,157,193,197]
N = 8
V, DEP = 32768, 16
def entries(a): return a.T.reshape(-1)
def pack(v, P): return np.ascontiguousarray(np.asarray(v, np.int32).reshape(-1, P).T)
def forest(rng, n, lev):
    P = np.arange(n)
    for l in range(1, int(lev.max()) + 1):
        a, b = np.nonzero(lev == l)[0], np.nonzero(lev == l - 1)[0]; P[a] = b[rng.integers(0, len(b), len(a))]
    return P
def lists(rng, how):
    n = N * V; P = np.arange(n)
    if how == "uniform":
        lev = rng.integers(0, DEP + 1, n); lev[rng.permutation(n)[:DEP + 1]] = np.arange(DEP + 1); P = forest(rng, n, lev)
    if how == "star":
        lev = np.ones(n, np.int64); lev[rng.permutation(n)[:4]] = 0; P = forest(rng, n, lev)
    if how == "chain":
        W = np.stack([V * r + rng.permutation(V)[:V // (DEP + 1) * (DEP + 1)].reshape(-1, DEP + 1) for r in range(N)]); P[W[:, :, 1:]] = np.roll(W, 1, axis=0)[:, :, :-1]
    if how == "deep":
        z = rng.permutation(N); g = V * z[1 + np.arange(DEP) % (N - 1)] + rng.permutation(V)[:DEP]; P[:] = g[-1]; P[g] = np.concatenate([g[:1], g[:-1]])
    if how == "whole":
        o = rng.permutation(N)
        for i in range(1, N - 1):
            if i % (DEP + 1): P[V * o[i]:V * o[i] + V] = V * o[i - 1] + rng.permutation(V)
        P[V * o[-1]:V * o[-1] + V] = V * o[-1] + forest(rng, V, rng.permutation(np.concatenate([np.arange(DEP + 1), rng.integers(0, DEP + 1, V - DEP - 1)])))
    return {"par": np.stack([pack(p, 16) for p in P.reshape(N, V)])}
def setup_inputs(rng):
    return dict({"val": rng.standard_normal((N, 16, V // 16), dtype=np.float32).astype(ml_dtypes.bfloat16)}, **lists(rng, "uniform"))
def setup_inputs_chain(rng):
    d = setup_inputs(rng); d.update(lists(rng, "chain"))
    for k in ("val",): d[k] = (d[k].astype(np.float32) * 1048576.0).astype(d[k].dtype)
    return d
def setup_inputs_deep(rng):
    d = setup_inputs(rng); d.update(lists(rng, "deep"))
    for k in ("val",): d[k] = (d[k].astype(np.float32) * (1 / 1024.0)).astype(d[k].dtype)
    return d
def setup_inputs_star(rng):
    d = setup_inputs(rng); d.update(lists(rng, "star"))
    return d
def setup_inputs_whole(rng):
    d = setup_inputs(rng); d.update(lists(rng, "whole"))
    return d
def check_inputs(x):
    bad = []
    if x["par"].min() < 0 or x["par"].max() >= N * V: bad.append("par out of range")
    p = np.concatenate([entries(a) for a in x["par"]]); q = p
    for k in range(DEP - 1): q = p[q]
    if (p[q] != q).any(): bad.append("a node is more than DEP hops from a root")
    return bad
def reference(val, par):
    p = np.concatenate([entries(a) for a in par]); v = np.concatenate([entries(a) for a in val])
    q = p
    for k in range(DEP - 1): q = p[q]
    return {"y": np.stack([np.ascontiguousarray(v[q][V * r:V * r + V].reshape(-1, 16).T) for r in range(N)])}

@@ -1,0 +1,365 @@
+from concourse.bass import DstId, RemoteDMATransfer
+from concourse.mybir import AluOpType as Op, ActivationFunctionType as Act
+
+NCORES = 256
+CHIPS_A_HOST = 8
+KC = 192 * 32768 - 16383
+HOPS = 16
+QCORES = CHIPS_A_HOST // 2 * 4
+KW = 256 // QCORES
+NCH = 2
+KB = KW // NCH
+L = 16 * KB
+
+SCRATCH = {
+    "tab": ("sbuf", [128, 16384], "float32"),
+    "vtab": ("sbuf", [128, 16384], "bfloat16"),
+    "land": ("dram", [1024, 256], "float32"),
+    "vland": ("dram", [1024, 256], "bfloat16"),
+    "pt": ("sbuf", [128, 256], "int32"),
+    "pa": ("sbuf", [128, 256], "int32"),
+    "pb": ("sbuf", [128, 256], "int32"),
+    "px": ("sbuf", [128, 256], "float32"),
+    "pw": ("sbuf", [128, 256], "float32"),
+    "d2": ("sbuf", [128, 256], "float32"),
+    "w2": ("sbuf", [128, 256], "float32"),
+    "vb": ("sbuf", [128, 256], "bfloat16"),
+    "m1": ("sbuf", [128, 128], "float32"),
+    "ccol": ("sbuf", [128, 8], "float32"),
+    "w1": ("sbuf", [128, KW], "float32"),
+    "ip": ("sbuf", [128, 8], "int32"),
+    "qi": ("sbuf", [128, 8], "int32"),
+    "bcol": ("sbuf", [128, 8], "float32"),
+    "ocol": ("sbuf", [128, 8], "float32"),
+    "di": ("sbuf", [128, L], "int32"),
+    "dj": ("sbuf", [128, L], "int32"),
+    "delta": ("sbuf", [128, L], "bfloat16"),
+    "so32": ("sbuf", [128, KB], "int32"),
+    "soff": ("sbuf", [128, KB], "uint16"),
+    "blkf": ("sbuf", [128, 128], "float32"),
+    "blkb": ("sbuf", [128, 128], "bfloat16"),
+    "yb": ("sbuf", [128, KW], "bfloat16"),
+    "ybuf": ("sbuf", [128, 256], "bfloat16"),
+}
+SEMAPHORES = ["fill", "vfill", "ls", "wsem", "ysem", "st"] + ["a%d" % i for i in range(8)] + ["b%d" % i for i in range(8)]
+SEMAPHORES += ["c%d" % i for i in range(40)]
+for _m in range(NCH):
+    SCRATCH["wr%d" % _m] = ("psum", [128, 512], "float32")
+    SCRATCH["row%d" % _m] = ("psum", [128, 512], "float32")
+    SCRATCH["e%d" % _m] = ("sbuf", [128, L], "bfloat16")
+    SCRATCH["mk%d" % _m] = ("sbuf", [128, L], "bfloat16")
+    SCRATCH["g%d" % _m] = ("sbuf", [128, L], "float32")
+    SCRATCH["gv%d" % _m] = ("sbuf", [128, L], "bfloat16")
+    SCRATCH["f%d" % _m] = ("sbuf", [128, KB], "int32")
+    SCRATCH["o%d" % _m] = ("sbuf", [128, KB], "int32")
+    SCRATCH["off%d" % _m] = ("sbuf", [128, KB], "uint16")
+    SEMAPHORES += [s + str(_m) for s in ("sW", "sE", "sR", "sM", "sO", "sG")]
+
+
+def layout(T, topo):
+    chips = {}
+    for c in range(NCORES):
+        chips.setdefault((topo.host(c), topo.chip(c)), []).append(c)
+    key = lambda c: (topo.host(c), topo.chip(c))
+    mate = {}
+    for a in chips:
+        for b in chips:
+            if topo.mates(chips[a][0], chips[b][0]):
+                mate[a] = b
+    ranks = list(T.cores)
+    work = []
+    for h in sorted(set(topo.host(c) for c in ranks)):
+        mine = []
+        for k in [key(c) for c in ranks if topo.host(c) == h] + [k for k in chips if k[0] == h]:
+            for x in (k, mate[k]):
+                if x not in mine and len(mine) < CHIPS_A_HOST:
+                    mine.append(x)
+        work += mine
+    qcores, sends, relay = [], {}, {}
+    gate = {}
+    for x in work:
+        for d in (0, 1):
+            far = [r for r, c in enumerate(ranks) if topo.die(c) == d and key(c) != x]
+            free = [c for c in chips[x] if topo.die(c) == d and c not in ranks]
+            for i, r in enumerate(far):
+                gate[(r, x)] = free[i % len(free)]
+    for r, c in enumerate(ranks):
+        d = topo.die(c)
+        q = [b for b in chips[key(c)] if topo.die(b) == d and b != c]
+        for x in work:
+            if x[0] == topo.host(c) and topo.same_plane(c, chips[x][0]):
+                q += [b for b in chips[x] if topo.die(b) == d]
+        qcores.append([c] + q)
+        team = [b for b in chips[key(c)] if topo.die(b) == d]
+        load = {b: (1 if b == c else 0) for b in team}
+        far = [x for x in work if x != key(c)]
+        far.sort(key=lambda x: sum(topo.may_write(b, gate[(r, x)]) for b in team))
+        for x in far:
+            b = min([b for b in team if topo.may_write(b, gate[(r, x)])], key=lambda b: load[b])
+            load[b] += 1
+            sends.setdefault(b, {}).setdefault(r, []).append(gate[(r, x)])
+    for (r, x), c in gate.items():
+        relay.setdefault(c, []).append(r)
+    return chips, key, work, qcores, sends, relay, gate
+
+
+def bits(m):
+    return [1 << i for i in range(16) if m >> i & 1]
+
+
+_cache = {}
+
+
+def rank_program(g, core, T, topo):
+    if "lay" not in _cache:
+        _cache["lay"] = layout(T, topo)
+    chips, key, work, qcores, sends, relay, gate = _cache["lay"]
+    if key(core) not in work:
+        return
+    ranks = list(T.cores)
+    rank = T.rank_of(core)
+    here = chips[key(core)]
+    V, S, PE, SY = g.vector, g.scalar, g.tensor, g.sync
+    owner = [r for r in range(8) if core in qcores[r]][0]
+    t = qcores[owner].index(core)
+    total = {}
+    nc = [0]
+
+    def inc(ins, name, n=1):
+        ins.then_inc(T.sem[name], n)
+        total[name] = total.get(name, 0) + n
+
+    def once(ins):
+        name = "c%d" % nc[0]
+        nc[0] += 1
+        inc(ins, name)
+        return name
+
+    def wait(q, name, n=1):
+        q.wait_ge(T.sem[name], n)
+
+    def dst(d):
+        rid, pid = topo.addr(d, core)
+        return DstId(rid=rid, pnc=pid)
+
+    def spread(src, buf, r, dsts, sem):
+        m = topo.mask(core, dsts[0])
+        n = len(bits(m))
+        g.remote_dma_fused([RemoteDMATransfer(dst_ids=[dst(d) for d in dsts], dma_engine_mask=m, remote_sem=T.sem[sem + str(r)],
+                                              srcs=[src], dsts=[buf[128 * r:128 * r + 128, :] for d in dsts])], local_sem=T.sem["ls"])
+        total["ls"] = total.get("ls", 0) + n
+
+    def arrives(r):
+        src = ranks[r]
+        if key(src) == key(core):
+            return len(bits(topo.mask(src, core)))
+        gw = gate[(r, key(core))]
+        if gw == core:
+            s = [b for b in sends if core in sends[b].get(r, [])][0]
+            return len(bits(topo.mask(s, core)))
+        return len(bits(topo.mask(gw, core)))
+
+    if rank is not None:
+        SY.dma_start(T.pt[:], T.par[:]).then_inc(T.sem["c38"], 16)
+        S.dma_start(T.vb[:], T.val[:]).then_inc(T.sem["c39"], 16)
+        total["c38"] = total["c39"] = 16
+        k = once(V.memset(T.m1[:], 0.0))
+        wait(g, k)
+        k = once(g.affine_select(T.m1[:], T.m1[:], [[-1, 128]], Op.not_equal, 1.0, 0, 1))
+        wait(g, k)
+        k = once(g.affine_select(T.m1[:], T.m1[:], [[-1, 128]], Op.not_equal, -1.0, 8, 1))
+        wait(g, k)
+        km1 = once(g.affine_select(T.m1[:], T.m1[:], [[-1, 128]], Op.not_equal, 1.0, -120, 1))
+        k = once(V.memset(T.ccol[:], 0.0))
+        wait(V, k)
+        kcc = once(V.memset(T.ccol[0:8, :], float(KC)))
+    k1 = once(V.memset(T.blkf[:], 1.0))
+    if rank is not None:
+        wait(V, "c38", 16)
+        ka = once(V.tensor_scalar(T.pa[:], T.pt[:], 15, None, Op.bitwise_and))
+        kb = once(V.tensor_scalar(T.pb[:], T.pt[:], 4, None, Op.logical_shift_right))
+        wait(V, ka)
+        kx = once(V.tensor_scalar(T.px[:], T.pa[:], 16384.0, None, Op.mult))
+        wait(V, kb)
+        wait(V, kx)
+        kw = once(V.tensor_tensor(T.pw[:], T.px[:], T.pb[:], Op.add))
+        wait(PE, km1)
+        wait(PE, kw)
+        kd = once(PE.matmul(T.wr0[:, 0:256], T.m1[:], T.pw[:], True, True))
+        wait(V, kcc)
+        wait(V, kd)
+        kd2 = once(V.tensor_scalar(T.d2[:], T.wr0[:, 0:256], T.ccol[:, 0:1], None, Op.add))
+        kw2 = once(V.tensor_scalar(T.w2[:], T.pw[:], 2.0, float(KC), Op.mult, Op.add))
+        near = [b for b in here if topo.die(b) == topo.die(core) and b != core]
+        cross = [b for b in here if topo.die(b) != topo.die(core)]
+        own = sends.get(core, {}).get(rank, [])
+        wait(g, kd2)
+        spread(T.d2[:], T.land, rank, near, "a")
+        if own:
+            spread(T.d2[:], T.land, rank, own, "a")
+        spread(T.d2[:], T.land, rank, cross, "a")
+
+    kip = once(g.iota(T.ip[:], [[0, 8]], 0, 1))
+    kdi = once(g.iota(T.di[:], [[0, KB], [-1, 16]], 16, 1))
+    kso = once(g.iota(T.so32[:], [[1, KB]], 0, 0))
+    wait(g, k1)
+    k = once(g.affine_select(T.blkf[:], T.blkf[:], [[-16, 8], [0, 16]], Op.is_ge, 0.0, 0, 1))
+    wait(g, k)
+    kblk = once(g.affine_select(T.blkf[:], T.blkf[:], [[16, 8], [0, 16]], Op.is_ge, 0.0, 15, -1))
+    wait(V, kip)
+    kq = once(V.tensor_scalar(T.qi[:], T.ip[:], 15, None, Op.bitwise_and))
+    wait(V, kdi)
+    kdj = once(V.tensor_scalar(T.dj[:], T.di[:], 15, None, Op.bitwise_and))
+    wait(V, kso)
+    ksf = once(V.tensor_copy(T.soff[:], T.so32[:]))
+    wait(V, kq)
+    kbc = once(V.tensor_scalar(T.bcol[:], T.qi[:], -32768.0, -191.5 * 32768, Op.mult, Op.add))
+    koc = once(V.tensor_scalar(T.ocol[:], T.qi[:], 32768.0, 192.0 * 32768, Op.mult, Op.add))
+    wait(V, kdj)
+    kdl = once(V.tensor_scalar(T.delta[:], T.dj[:], 0.0, None, Op.is_equal))
+    wait(V, kblk)
+    kbb = once(V.tensor_copy(T.blkb[:], T.blkf[:]))
+
+    if rank is not None:
+        wait(g, kw2)
+        near = [b for b in qcores[rank] if key(b) == key(core) and b != core]
+        far = [b for b in qcores[rank] if key(b) != key(core)]
+        calls = [(near, 4)] + [(far[i:i + 4], 2) for i in range(0, len(far), 4)]
+        for dsts, n in calls:
+            tr = []
+            for i, d in enumerate(dsts):
+                j = qcores[rank].index(d)
+                tr.append(RemoteDMATransfer(dst_ids=[dst(d)], dma_engine_mask=sum(bits(topo.mask(core, d))[n * i:n * i + n]),
+                                            remote_sem=T.sem["wsem"], srcs=[T.w2[:, KW * j:KW * j + KW]], dsts=[T.w1[:]]))
+            g.remote_dma_fused(tr, local_sem=T.sem["ls"])
+            total["ls"] += n * len(dsts)
+    rest = [b for b in here if b != core]
+    for sem, buf in (("a", T.land), ("b", T.vland)):
+        if rank is not None:
+            if sem == "b":
+                wait(g, "c39", 16)
+                spread(T.vb[:], buf, rank, [b for b in here if topo.die(b) == topo.die(core) and b != core], sem)
+                if own:
+                    spread(T.vb[:], buf, rank, own, sem)
+                spread(T.vb[:], buf, rank, [b for b in here if topo.die(b) != topo.die(core)], sem)
+            continue
+        for r, dsts in sends.get(core, {}).items():
+            wait(g, sem + str(r), arrives(r))
+            spread(buf[128 * r:128 * r + 128, :], buf, r, dsts, sem)
+        for r in relay.get(core, []):
+            wait(g, sem + str(r), arrives(r))
+            spread(buf[128 * r:128 * r + 128, :], buf, r, rest, sem)
+
+    def near_rank(r):
+        c = ranks[r]
+        if c == core:
+            return 0
+        if key(c) == key(core):
+            return 1 if topo.die(c) == topo.die(core) else 2
+        if topo.same_plane(c, core):
+            return 3
+        return 4
+
+    order = sorted(range(8), key=near_rank)
+    for r in order:
+        for q, gs in ((SY, range(0, 4)), (S, range(4, 8))):
+            if r == rank:
+                wait(q, kd2)
+                src = T.d2[:]
+            else:
+                wait(q, "a%d" % r, arrives(r))
+                total["a%d" % r] = arrives(r)
+                src = T.land[128 * r:128 * r + 128, :]
+            for i in gs:
+                inc(q.dma_start(T.tab[16 * i:16 * i + 16, 2048 * r:2048 * r + 2048], src), "fill", 16)
+    for r in order:
+        if r == rank:
+            wait(SY, "c39", 16)
+            src = T.vb[:]
+        else:
+            wait(SY, "b%d" % r, arrives(r))
+            total["b%d" % r] = arrives(r)
+            src = T.vland[128 * r:128 * r + 128, :]
+        for i in range(8):
+            inc(SY.dma_start(T.vtab[16 * i:16 * i + 16, 2048 * r:2048 * r + 2048], src), "vfill", 16)
+
+    if rank is None:
+        nw = 4 if key(core) == key(ranks[owner]) else 2
+        total["wsem"] = nw
+        wait(V, "wsem", nw)
+        first = T.w1
+    else:
+        wait(V, kw2)
+        first = T.w2
+    wait(V, ksf)
+    wait(V, kdl)
+    wait(PE, kbb)
+    wait(PE, kblk)
+    wait(S, kbc)
+    ybase = T.ybuf if rank is not None else T.yb
+    for h in range(HOPS):
+        last = h == HOPS - 1
+        for m in range(NCH):
+            n = str(m)
+            wr, row, e, mk, G, f, o, off = (T[x + n] for x in ("wr", "row", "e", "mk", "g", "f", "o", "off"))
+            if h == 0:
+                w = first[:, KB * m:KB * m + KB]
+                inc(V.tensor_tensor(e[:], w.indirect(T.soff[:, 0:KB]), T.delta[:], Op.mult), "sE" + n)
+                inc(V.tensor_scalar(f[:], w, 16383.0, 0.5, Op.add, Op.mult), "sO" + n)
+            else:
+                wait(V, "sW" + n, h)
+                inc(V.tensor_tensor(e[:], wr[:, 0:L], T.delta[:], Op.mult), "sE" + n)
+                inc(V.tensor_scalar(f[:], wr[:, 0:L:16], 16383.0, 0.5, Op.add, Op.mult), "sO" + n)
+            wait(V, "sO" + n, 3 * h + 1)
+            inc(V.tensor_scalar(o[:], f[:], 16383, None, Op.bitwise_and), "sO" + n)
+            wait(V, "sO" + n, 3 * h + 2)
+            inc(V.tensor_copy(off[:], o[:]), "sO" + n)
+            wait(PE, "sE" + n, h + 1)
+            inc(PE.matmul(row[:, 0:L], T.blkb[:], e[:], True, True), "sR" + n)
+            if not last:
+                wait(S, "sR" + n, h + 1)
+                inc(S.activation(mk[:], row[:, 0:L], Act.Sign, bias=T.bcol[:, 0:1]), "sM" + n)
+            wait(V, "sO" + n, 3 * h + 3)
+            if not last:
+                if h == 0 and m == 0:
+                    wait(V, "fill", 1024)
+                wait(V, "sM" + n, h + 1)
+                inc(V.tensor_tensor(G[:], T.tab[:, 0:16384].indirect(off[:, 0:KB]), mk[:], Op.mult), "sG" + n)
+            else:
+                wait(V, koc)
+                wait(V, "sR" + n, h + 1)
+                inc(V.tensor_scalar(mk[:], row[:, 0:L], T.ocol[:, 0:1], None, Op.is_equal), "sM" + n)
+                wait(V, "sM" + n, h + 1)
+                if m == 0:
+                    wait(V, "vfill", 1024)
+                G = T["gv" + n]
+                inc(V.tensor_tensor(G[:], T.vtab[:, 0:16384].indirect(off[:, 0:KB]), mk[:], Op.mult), "sG" + n)
+            wait(PE, "sG" + n, h + 1)
+            for i in range(L // 128):
+                lhs = G[:, 128 * i:128 * i + 128]
+                if not last:
+                    ins = PE.matmul(wr[:, 128 * i:128 * i + 128], lhs, T.blkf[:], True, True)
+                else:
+                    ins = PE.matmul(wr[:, 8 * i:8 * i + 8], lhs, T.blkb[:, 0:128:16], True, True)
+                if i == L // 128 - 1:
+                    inc(ins, "sW" + n)
+    ky = []
+    for m in range(NCH):
+        wait(V, "sW%d" % m, HOPS)
+        ky.append(once(V.tensor_copy(ybase[:, KB * m:KB * m + KB], T["wr%d" % m][:, 0:KB])))
+
+    if rank is None:
+        for k in ky:
+            wait(g, k)
+        d = ranks[owner]
+        m = sum(bits(topo.mask(core, d))[:8])
+        g.remote_dma(T.ybuf[:, KW * t:KW * t + KW], T.yb[:], T.sem["ysem"], T.sem["ls"], topo.addr(d, core)[1], topo.addr(d, core)[0], m)
+        total["ls"] = total.get("ls", 0) + 8
+    else:
+        total["ysem"] = 8 * (QCORES - 1)
+        for k in ky:
+            wait(SY, k)
+        wait(SY, "ysem", total["ysem"])
+        inc(SY.dma_start(T.y[:], T.ybuf[:]), "st", 16)
+    for name, n in total.items():
+        wait(g, name, n)

@@ -10,22 +10,26 @@ KW = 256 // QCORES
 NCH = 2
 KB = KW // NCH
 L = 16 * KB
+H = L // 2
 
 SCRATCH = {
     "tab": ("sbuf", [128, 16384], "float32"),
     "vtab": ("sbuf", [128, 16384], "bfloat16"),
-    "land": ("dram", [1024, 256], "float32"),
+    "sp": ("sbuf", [128, 4096], "float16"),
+    "land": ("dram", [1024, 512], "float16"),
     "vland": ("dram", [1024, 256], "bfloat16"),
     "pt": ("sbuf", [128, 256], "int32"),
     "pa": ("sbuf", [128, 256], "int32"),
     "pb": ("sbuf", [128, 256], "int32"),
     "px": ("sbuf", [128, 256], "float32"),
     "pw": ("sbuf", [128, 256], "float32"),
-    "d2": ("sbuf", [128, 256], "float32"),
     "w2": ("sbuf", [128, 256], "float32"),
     "vb": ("sbuf", [128, 256], "bfloat16"),
-    "m1": ("sbuf", [128, 128], "float32"),
-    "ccol": ("sbuf", [128, 8], "float32"),
+    "m1": ("sbuf", [128, 256], "float32"),
+    "ri": ("sbuf", [128, 512], "int32"),
+    "rj": ("sbuf", [128, 512], "int32"),
+    "rep": ("sbuf", [128, 512], "float16"),
+    "kcol": ("sbuf", [128, 8], "float32"),
     "w1": ("sbuf", [128, KW], "float32"),
     "ip": ("sbuf", [128, 8], "int32"),
     "qi": ("sbuf", [128, 8], "int32"),
@@ -34,15 +38,21 @@ SCRATCH = {
     "di": ("sbuf", [128, L], "int32"),
     "dj": ("sbuf", [128, L], "int32"),
     "delta": ("sbuf", [128, L], "bfloat16"),
-    "so32": ("sbuf", [128, KB], "int32"),
-    "soff": ("sbuf", [128, KB], "uint16"),
+    "so32": ("sbuf", [128, 8], "int32"),
+    "sb32": ("sbuf", [128, 8], "int32"),
+    "sc32": ("sbuf", [128, 8], "int32"),
+    "soff": ("sbuf", [128, 8], "uint16"),
     "blkf": ("sbuf", [128, 128], "float32"),
     "blkb": ("sbuf", [128, 128], "bfloat16"),
     "yb": ("sbuf", [128, KW], "bfloat16"),
     "ybuf": ("sbuf", [128, 256], "bfloat16"),
 }
-SEMAPHORES = ["fill", "vfill", "ls", "wsem", "ysem", "st"] + ["a%d" % i for i in range(8)] + ["b%d" % i for i in range(8)]
-SEMAPHORES += ["c%d" % i for i in range(40)]
+SEMAPHORES = ["vfill", "ls", "wsem", "ysem", "st"]
+for _m in range(8):
+    SEMAPHORES += [s + str(_m) for s in ("a", "b", "l")]
+for _m in range(4):
+    SEMAPHORES += ["pf%d" % _m, "ev%d" % _m]
+SEMAPHORES += ["c%d" % i for i in range(44)]
 for _m in range(NCH):
     SCRATCH["wr%d" % _m] = ("psum", [128, 512], "float32")
     SCRATCH["row%d" % _m] = ("psum", [128, 512], "float32")
@@ -142,12 +152,27 @@ def rank_program(g, core, T, topo):
         rid, pid = topo.addr(d, core)
         return DstId(rid=rid, pnc=pid)
 
-    def spread(src, buf, r, dsts, sem):
+    def sends_on(c, r):
+        return c != ranks[r] and (r in sends.get(c, {}) or r in relay.get(c, []))
+
+    def piece(r):
+        return T.sp[:, 512 * r:512 * r + 512]
+
+    def stored(r):
+        return T.land[128 * r:128 * r + 128, :]
+
+    def vstored(r):
+        return T.vland[128 * r:128 * r + 128, :]
+
+    def spread(src, sem, r, dsts):
         m = topo.mask(core, dsts[0])
-        n = len(bits(m))
+        if sem == "a":
+            out = [stored(r) if sends_on(d, r) else piece(r) for d in dsts]
+        else:
+            out = [vstored(r) for d in dsts]
         g.remote_dma_fused([RemoteDMATransfer(dst_ids=[dst(d) for d in dsts], dma_engine_mask=m, remote_sem=T.sem[sem + str(r)],
-                                              srcs=[src], dsts=[buf[128 * r:128 * r + 128, :] for d in dsts])], local_sem=T.sem["ls"])
-        total["ls"] = total.get("ls", 0) + n
+                                              srcs=[src], dsts=out)], local_sem=T.sem["ls"])
+        total["ls"] = total.get("ls", 0) + len(bits(m))
 
     def arrives(r):
         src = ranks[r]
@@ -159,23 +184,34 @@ def rank_program(g, core, T, topo):
             return len(bits(topo.mask(s, core)))
         return len(bits(topo.mask(gw, core)))
 
-    if rank is not None:
-        SY.dma_start(T.pt[:], T.par[:]).then_inc(T.sem["c38"], 16)
-        S.dma_start(T.vb[:], T.val[:]).then_inc(T.sem["c39"], 16)
-        total["c38"] = total["c39"] = 16
-        k = once(V.memset(T.m1[:], 0.0))
-        wait(g, k)
-        k = once(g.affine_select(T.m1[:], T.m1[:], [[-1, 128]], Op.not_equal, 1.0, 0, 1))
-        wait(g, k)
-        k = once(g.affine_select(T.m1[:], T.m1[:], [[-1, 128]], Op.not_equal, -1.0, 8, 1))
-        wait(g, k)
-        km1 = once(g.affine_select(T.m1[:], T.m1[:], [[-1, 128]], Op.not_equal, 1.0, -120, 1))
-        k = once(V.memset(T.ccol[:], 0.0))
-        wait(V, k)
-        kcc = once(V.memset(T.ccol[0:8, :], float(KC)))
+    near = [b for b in here if topo.die(b) == topo.die(core) and b != core]
+    cross = [b for b in here if topo.die(b) != topo.die(core)]
+    own = sends.get(core, {}).get(rank, [])
+
     k1 = once(V.memset(T.blkf[:], 1.0))
     if rank is not None:
-        wait(V, "c38", 16)
+        SY.dma_start(T.pt[:], T.par[:]).then_inc(T.sem["c42"], 16)
+        S.dma_start(T.vb[:], T.val[:]).then_inc(T.sem["c43"], 16)
+        total["c42"] = total["c43"] = 16
+        k = once(V.memset(T.m1[:], 0.0))
+        wait(g, k)
+        pat = [[-1, 2], [0, 2], [-2, 64]]
+        k = once(g.affine_select(T.m1[:], T.m1[:], pat, Op.not_equal, 0.0625, 0, 1))
+        wait(g, k)
+        k = once(g.affine_select(T.m1[:], T.m1[:], pat, Op.not_equal, -0.0625, 8, 1))
+        wait(g, k)
+        km1 = once(g.affine_select(T.m1[:], T.m1[:], pat, Op.not_equal, 0.0625, -120, 1))
+    kip = once(g.iota(T.ip[:], [[0, 8]], 0, 1))
+    kri = once(g.iota(T.ri[:], [[-1, 4], [0, 8], [-4, 16]], 64, 1))
+    kdi = once(g.iota(T.di[:], [[-1, 2], [0, KB], [-2, 8]], 16, 1))
+    kso = once(g.iota(T.so32[:], [[2, 8]], 0, 0))
+    wait(g, k1)
+    k = once(g.affine_select(T.blkf[:], T.blkf[:], [[-16, 8], [0, 16]], Op.is_ge, 0.0, 0, 1))
+    wait(g, k)
+    kblk = once(g.affine_select(T.blkf[:], T.blkf[:], [[16, 8], [0, 16]], Op.is_ge, 0.0, 15, -1))
+
+    if rank is not None:
+        wait(V, "c42", 16)
         ka = once(V.tensor_scalar(T.pa[:], T.pt[:], 15, None, Op.bitwise_and))
         kb = once(V.tensor_scalar(T.pb[:], T.pt[:], 4, None, Op.logical_shift_right))
         wait(V, ka)
@@ -185,46 +221,50 @@ def rank_program(g, core, T, topo):
         kw = once(V.tensor_tensor(T.pw[:], T.px[:], T.pb[:], Op.add))
         wait(PE, km1)
         wait(PE, kw)
-        kd = once(PE.matmul(T.wr0[:, 0:256], T.m1[:], T.pw[:], True, True))
-        wait(V, kcc)
-        wait(V, kd)
-        kd2 = once(V.tensor_scalar(T.d2[:], T.wr0[:, 0:256], T.ccol[:, 0:1], None, Op.add))
+        PE.matmul(T.wr0[:, 0:256], T.m1[:, 0:128], T.pw[:], True, True)
+        kd = once(PE.matmul(T.wr0[:, 256:512], T.m1[:, 128:256], T.pw[:], True, True))
+        wait(V, kw)
         kw2 = once(V.tensor_scalar(T.w2[:], T.pw[:], 2.0, float(KC), Op.mult, Op.add))
-        near = [b for b in here if topo.die(b) == topo.die(core) and b != core]
-        cross = [b for b in here if topo.die(b) != topo.die(core)]
-        own = sends.get(core, {}).get(rank, [])
+        wait(V, kd)
+        kh = once(V.tensor_copy(piece(rank), T.wr0[:, 0:512]))
+        wait(V, kh)
+        lo = T.sp[64:128, 512 * rank:512 * rank + 512]
+        kd2 = once(V.tensor_tensor(lo, T.wr0[64:128, 0:512], lo, Op.subtract))
+        wait(g, kh)
         wait(g, kd2)
-        spread(T.d2[:], T.land, rank, near, "a")
+        spread(piece(rank), "a", rank, near)
         if own:
-            spread(T.d2[:], T.land, rank, own, "a")
-        spread(T.d2[:], T.land, rank, cross, "a")
+            spread(piece(rank), "a", rank, own)
+        spread(piece(rank), "a", rank, cross)
 
-    kip = once(g.iota(T.ip[:], [[0, 8]], 0, 1))
-    kdi = once(g.iota(T.di[:], [[0, KB], [-1, 16]], 16, 1))
-    kso = once(g.iota(T.so32[:], [[1, KB]], 0, 0))
-    wait(g, k1)
-    k = once(g.affine_select(T.blkf[:], T.blkf[:], [[-16, 8], [0, 16]], Op.is_ge, 0.0, 0, 1))
-    wait(g, k)
-    kblk = once(g.affine_select(T.blkf[:], T.blkf[:], [[16, 8], [0, 16]], Op.is_ge, 0.0, 15, -1))
     wait(V, kip)
     kq = once(V.tensor_scalar(T.qi[:], T.ip[:], 15, None, Op.bitwise_and))
+    ks1 = once(V.tensor_scalar(T.sb32[:], T.ip[:], 3, 1, Op.logical_shift_right, Op.bitwise_and))
+    wait(V, kri)
+    krj = once(V.tensor_scalar(T.rj[:], T.ri[:], 63, None, Op.bitwise_and))
+    wait(V, kq)
+    kkc = once(V.tensor_scalar(T.kcol[:], T.qi[:], 0.0, float(KC), Op.is_equal, Op.mult))
+    kbc = once(V.tensor_scalar(T.bcol[:], T.qi[:], -32768.0, -191.5 * 32768, Op.mult, Op.add))
+    koc = once(V.tensor_scalar(T.ocol[:], T.qi[:], 32768.0, 192.0 * 32768, Op.mult, Op.add))
+    wait(V, krj)
+    krp = once(V.tensor_scalar(T.rep[:], T.rj[:], 0.0, 16.0, Op.is_equal, Op.mult))
     wait(V, kdi)
     kdj = once(V.tensor_scalar(T.dj[:], T.di[:], 15, None, Op.bitwise_and))
     wait(V, kso)
-    ksf = once(V.tensor_copy(T.soff[:], T.so32[:]))
-    wait(V, kq)
-    kbc = once(V.tensor_scalar(T.bcol[:], T.qi[:], -32768.0, -191.5 * 32768, Op.mult, Op.add))
-    koc = once(V.tensor_scalar(T.ocol[:], T.qi[:], 32768.0, 192.0 * 32768, Op.mult, Op.add))
+    wait(V, ks1)
+    ks2 = once(V.tensor_tensor(T.sc32[:], T.so32[:], T.sb32[:], Op.add))
     wait(V, kdj)
     kdl = once(V.tensor_scalar(T.delta[:], T.dj[:], 0.0, None, Op.is_equal))
+    wait(V, ks2)
+    ksf = once(V.tensor_copy(T.soff[:], T.sc32[:]))
     wait(V, kblk)
     kbb = once(V.tensor_copy(T.blkb[:], T.blkf[:]))
 
     if rank is not None:
         wait(g, kw2)
-        near = [b for b in qcores[rank] if key(b) == key(core) and b != core]
+        qn = [b for b in qcores[rank] if key(b) == key(core) and b != core]
         far = [b for b in qcores[rank] if key(b) != key(core)]
-        calls = [(near, 4)] + [(far[i:i + 4], 2) for i in range(0, len(far), 4)]
+        calls = [(qn, 4)] + [(far[i:i + 4], 2) for i in range(0, len(far), 4)]
         for dsts, n in calls:
             tr = []
             for i, d in enumerate(dsts):
@@ -233,22 +273,20 @@ def rank_program(g, core, T, topo):
                                             remote_sem=T.sem["wsem"], srcs=[T.w2[:, KW * j:KW * j + KW]], dsts=[T.w1[:]]))
             g.remote_dma_fused(tr, local_sem=T.sem["ls"])
             total["ls"] += n * len(dsts)
-    rest = [b for b in here if b != core]
-    for sem, buf in (("a", T.land), ("b", T.vland)):
-        if rank is not None:
-            if sem == "b":
-                wait(g, "c39", 16)
-                spread(T.vb[:], buf, rank, [b for b in here if topo.die(b) == topo.die(core) and b != core], sem)
-                if own:
-                    spread(T.vb[:], buf, rank, own, sem)
-                spread(T.vb[:], buf, rank, [b for b in here if topo.die(b) != topo.die(core)], sem)
-            continue
-        for r, dsts in sends.get(core, {}).items():
-            wait(g, sem + str(r), arrives(r))
-            spread(buf[128 * r:128 * r + 128, :], buf, r, dsts, sem)
-        for r in relay.get(core, []):
-            wait(g, sem + str(r), arrives(r))
-            spread(buf[128 * r:128 * r + 128, :], buf, r, rest, sem)
+        wait(g, "c43", 16)
+        spread(T.vb[:], "b", rank, near)
+        if own:
+            spread(T.vb[:], "b", rank, own)
+        spread(T.vb[:], "b", rank, cross)
+    else:
+        rest = [b for b in here if b != core]
+        for sem, src in (("a", stored), ("b", vstored)):
+            for r, dsts in sends.get(core, {}).items():
+                wait(g, sem + str(r), arrives(r))
+                spread(src(r), sem, r, dsts)
+            for r in relay.get(core, []):
+                wait(g, sem + str(r), arrives(r))
+                spread(src(r), sem, r, rest)
 
     def near_rank(r):
         c = ranks[r]
@@ -261,25 +299,44 @@ def rank_program(g, core, T, topo):
         return 4
 
     order = sorted(range(8), key=near_rank)
-    for r in order:
-        for q, gs in ((SY, range(0, 4)), (S, range(4, 8))):
-            if r == rank:
-                wait(q, kd2)
-                src = T.d2[:]
+    banks = [T.wr0, T.row0, T.wr1, T.row1]
+    wait(PE, krp)
+    wait(S, kkc)
+    wait(V, kkc)
+    for i, r in enumerate(order):
+        if r == rank:
+            wait(PE, kh)
+            wait(PE, kd2)
+        elif sends_on(core, r):
+            wait(SY, "a%d" % r, arrives(r))
+            total["a%d" % r] = arrives(r)
+            inc(SY.dma_start(piece(r), stored(r)), "l%d" % r, 16)
+            wait(PE, "l%d" % r, 16)
+        else:
+            wait(PE, "a%d" % r, arrives(r))
+            total["a%d" % r] = arrives(r)
+        for cb in range(4):
+            n = str(cb)
+            if i:
+                wait(PE, "ev" + n, i)
+            inc(PE.matmul(banks[cb][:, 0:512], T.rep[:, 128 * cb:128 * cb + 128], piece(r), True, True), "pf" + n)
+            out = T.tab[:, 2048 * r + 512 * cb:2048 * r + 512 * cb + 512]
+            if cb % 2 == 0:
+                wait(V, "pf" + n, i + 1)
+                inc(V.tensor_scalar(out, banks[cb][:, 0:512], T.kcol[:, 0:1], None, Op.add), "ev" + n)
             else:
-                wait(q, "a%d" % r, arrives(r))
-                total["a%d" % r] = arrives(r)
-                src = T.land[128 * r:128 * r + 128, :]
-            for i in gs:
-                inc(q.dma_start(T.tab[16 * i:16 * i + 16, 2048 * r:2048 * r + 2048], src), "fill", 16)
+                wait(S, "pf" + n, i + 1)
+                inc(S.activation(out, banks[cb][:, 0:512], Act.Identity, bias=T.kcol[:, 0:1]), "ev" + n)
+    for cb in range(4):
+        wait(PE, "ev%d" % cb, 8)
     for r in order:
         if r == rank:
-            wait(SY, "c39", 16)
+            wait(SY, "c43", 16)
             src = T.vb[:]
         else:
             wait(SY, "b%d" % r, arrives(r))
             total["b%d" % r] = arrives(r)
-            src = T.vland[128 * r:128 * r + 128, :]
+            src = vstored(r)
         for i in range(8):
             inc(SY.dma_start(T.vtab[16 * i:16 * i + 16, 2048 * r:2048 * r + 2048], src), "vfill", 16)
 
@@ -304,17 +361,19 @@ def rank_program(g, core, T, topo):
             wr, row, e, mk, G, f, o, off = (T[x + n] for x in ("wr", "row", "e", "mk", "g", "f", "o", "off"))
             if h == 0:
                 w = first[:, KB * m:KB * m + KB]
-                inc(V.tensor_tensor(e[:], w.indirect(T.soff[:, 0:KB]), T.delta[:], Op.mult), "sE" + n)
+                for u in range(2):
+                    inc(V.tensor_tensor(e[:, u:L:2], w.indirect(T.soff[:, 0:KB // 2]), T.delta[:, H * u:H * u + H], Op.mult), "sE" + n)
                 inc(V.tensor_scalar(f[:], w, 16383.0, 0.5, Op.add, Op.mult), "sO" + n)
             else:
                 wait(V, "sW" + n, h)
-                inc(V.tensor_tensor(e[:], wr[:, 0:L], T.delta[:], Op.mult), "sE" + n)
-                inc(V.tensor_scalar(f[:], wr[:, 0:L:16], 16383.0, 0.5, Op.add, Op.mult), "sO" + n)
+                for u in range(2):
+                    inc(V.tensor_tensor(e[:, u:L:2], wr[:, 0:H], T.delta[:, H * u:H * u + H], Op.mult), "sE" + n)
+                inc(V.tensor_scalar(f[:], wr[:, 0:H:8], 16383.0, 0.5, Op.add, Op.mult), "sO" + n)
             wait(V, "sO" + n, 3 * h + 1)
             inc(V.tensor_scalar(o[:], f[:], 16383, None, Op.bitwise_and), "sO" + n)
             wait(V, "sO" + n, 3 * h + 2)
             inc(V.tensor_copy(off[:], o[:]), "sO" + n)
-            wait(PE, "sE" + n, h + 1)
+            wait(PE, "sE" + n, 2 * h + 2)
             inc(PE.matmul(row[:, 0:L], T.blkb[:], e[:], True, True), "sR" + n)
             if not last:
                 wait(S, "sR" + n, h + 1)
@@ -322,7 +381,8 @@ def rank_program(g, core, T, topo):
             wait(V, "sO" + n, 3 * h + 3)
             if not last:
                 if h == 0 and m == 0:
-                    wait(V, "fill", 1024)
+                    for cb in range(4):
+                        wait(V, "ev%d" % cb, 8)
                 wait(V, "sM" + n, h + 1)
                 inc(V.tensor_tensor(G[:], T.tab[:, 0:16384].indirect(off[:, 0:KB]), mk[:], Op.mult), "sG" + n)
             else:
@@ -338,7 +398,7 @@ def rank_program(g, core, T, topo):
             for i in range(L // 128):
                 lhs = G[:, 128 * i:128 * i + 128]
                 if not last:
-                    ins = PE.matmul(wr[:, 128 * i:128 * i + 128], lhs, T.blkf[:], True, True)
+                    ins = PE.matmul(wr[:, 64 * i:64 * i + 64], lhs, T.blkf[:, 0:128:2], True, True)
                 else:
                     ins = PE.matmul(wr[:, 8 * i:8 * i + 8], lhs, T.blkb[:, 0:128:16], True, True)
                 if i == L // 128 - 1:

@@ -44,10 +44,13 @@ SCRATCH = {
     "soff": ("sbuf", [128, 8], "uint16"),
     "blkf": ("sbuf", [128, 128], "float32"),
     "blkb": ("sbuf", [128, 128], "bfloat16"),
+    "fi": ("sbuf", [128, KW], "int32"),
+    "oi": ("sbuf", [128, KW], "int32"),
+    "offs": ("sbuf", [128, KW], "uint16"),
     "yb": ("sbuf", [128, KW], "bfloat16"),
     "ybuf": ("sbuf", [128, 256], "bfloat16"),
 }
-SEMAPHORES = ["vfill", "ls", "wsem", "ysem", "st"]
+SEMAPHORES = ["sO", "vfill", "ls", "wsem", "ysem", "st"]
 for _m in range(8):
     SEMAPHORES += [s + str(_m) for s in ("a", "b", "l")]
 for _m in range(4):
@@ -60,10 +63,7 @@ for _m in range(NCH):
     SCRATCH["mk%d" % _m] = ("sbuf", [128, L], "bfloat16")
     SCRATCH["g%d" % _m] = ("sbuf", [128, L], "float32")
     SCRATCH["gv%d" % _m] = ("sbuf", [128, L], "bfloat16")
-    SCRATCH["f%d" % _m] = ("sbuf", [128, KB], "int32")
-    SCRATCH["o%d" % _m] = ("sbuf", [128, KB], "int32")
-    SCRATCH["off%d" % _m] = ("sbuf", [128, KB], "uint16")
-    SEMAPHORES += [s + str(_m) for s in ("sW", "sE", "sR", "sM", "sO", "sG")]
+    SEMAPHORES += [s + str(_m) for s in ("sW", "sE", "sR", "sM", "sG")]
 
 
 def layout(T, topo):
@@ -77,6 +77,7 @@ def layout(T, topo):
             if topo.mates(chips[a][0], chips[b][0]):
                 mate[a] = b
     ranks = list(T.cores)
+    homes = set(key(c) for c in ranks)
     work = []
     for h in sorted(set(topo.host(c) for c in ranks)):
         mine = []
@@ -85,14 +86,38 @@ def layout(T, topo):
                 if x not in mine and len(mine) < CHIPS_A_HOST:
                     mine.append(x)
         work += mine
-    qcores, sends, relay = [], {}, {}
-    gate = {}
+    free = []
     for x in work:
-        for d in (0, 1):
-            far = [r for r, c in enumerate(ranks) if topo.die(c) == d and key(c) != x]
-            free = [c for c in chips[x] if topo.die(c) == d and c not in ranks]
-            for i, r in enumerate(far):
-                gate[(r, x)] = free[i % len(free)]
+        if x not in homes and mate[x] not in homes and mate[x] not in free:
+            free.append(x)
+    entry = {}
+    for r, c in enumerate(ranks):
+        for x in work:
+            if x == key(c):
+                continue
+            if x == mate[key(c)]:
+                entry[(r, x)] = x
+                continue
+            near = x if topo.same_plane(c, chips[x][0]) else mate[x]
+            pair = x if x in free else mate[x]
+            over = pair in free and (free.index(pair) + topo.host(c)) % 2 == 0
+            entry[(r, x)] = mate[near] if over else near
+    sends, relay, gate, load = {}, {}, {}, {}
+    for x in work:
+        for first in (True, False):
+            for r, c in enumerate(ranks):
+                if x == key(c) or (entry[(r, x)] == x) != first:
+                    continue
+                can = [b for b in chips[x] if topo.die(b) == topo.die(c) and b not in ranks]
+                owns = [b for b in can if topo.may_write(b, chips[mate[x]][0])]
+                if first and x != mate[key(c)]:
+                    can = owns
+                elif first:
+                    can = [b for b in can if b not in owns]
+                b = min(can, key=lambda b: load.get(b, 0))
+                gate[(r, x)] = b
+                load[b] = load.get(b, 0) + 1
+    qcores = []
     for r, c in enumerate(ranks):
         d = topo.die(c)
         q = [b for b in chips[key(c)] if topo.die(b) == d and b != c]
@@ -101,16 +126,44 @@ def layout(T, topo):
                 q += [b for b in chips[x] if topo.die(b) == d]
         qcores.append([c] + q)
         team = [b for b in chips[key(c)] if topo.die(b) == d]
-        load = {b: (1 if b == c else 0) for b in team}
-        far = [x for x in work if x != key(c)]
-        far.sort(key=lambda x: sum(topo.may_write(b, gate[(r, x)]) for b in team))
+        far = [x for x in work if x != key(c) and entry[(r, x)] == x]
+        far.sort(key=lambda x: (sum(topo.may_write(b, gate[(r, x)]) for b in team), x == mate[key(c)]))
+        load[c] = 1
         for x in far:
-            b = min([b for b in team if topo.may_write(b, gate[(r, x)])], key=lambda b: load[b])
-            load[b] += 1
+            b = min([b for b in team if topo.may_write(b, gate[(r, x)])], key=lambda b: load.get(b, 0))
+            load[b] = load.get(b, 0) + 1
             sends.setdefault(b, {}).setdefault(r, []).append(gate[(r, x)])
-    for (r, x), c in gate.items():
-        relay.setdefault(c, []).append(r)
-    return chips, key, work, qcores, sends, relay, gate
+    come, at = {}, {}
+    for r, c in enumerate(ranks):
+        at[(c, r)] = 0
+        for b in chips[key(c)]:
+            if b != c:
+                come[(b, r)] = c
+                at[(b, r)] = 4 if topo.die(b) == topo.die(c) else 8
+    for r, c in enumerate(ranks):
+        for b in sends:
+            for i, y in enumerate(sends[b].get(r, [])):
+                come[(y, r)] = b
+                at[(y, r)] = at[(b, r)] + (6 if b == c else 4) + i
+    for first in (True, False):
+        for x in work:
+            ways = sorted((at.get((gate[(r, x)], r), 0), r) for r, c in enumerate(ranks)
+                          if x != key(c) and (entry[(r, x)] == x) == first)
+            for _, r in ways:
+                c, y = ranks[r], gate[(r, x)]
+                if not first:
+                    o = gate[(r, mate[x])]
+                    come[(y, r)] = o
+                    at[(y, r)] = at[(o, r)] + 4
+                n = gate[(r, mate[x])] if first and x != mate[key(c)] else None
+                relay.setdefault(y, []).append((r, n))
+                for b in chips[x]:
+                    if b != y:
+                        come[(b, r)] = y
+                        at[(b, r)] = at[(y, r)] + (7 if n is not None else 6)
+    for c in relay:
+        relay[c].sort(key=lambda p: at[(c, p[0])])
+    return chips, key, work, qcores, sends, relay, come, at
 
 
 def bits(m):
@@ -123,7 +176,7 @@ _cache = {}
 def rank_program(g, core, T, topo):
     if "lay" not in _cache:
         _cache["lay"] = layout(T, topo)
-    chips, key, work, qcores, sends, relay, gate = _cache["lay"]
+    chips, key, work, qcores, sends, relay, come, at = _cache["lay"]
     if key(core) not in work:
         return
     ranks = list(T.cores)
@@ -153,7 +206,7 @@ def rank_program(g, core, T, topo):
         return DstId(rid=rid, pnc=pid)
 
     def sends_on(c, r):
-        return c != ranks[r] and (r in sends.get(c, {}) or r in relay.get(c, []))
+        return c != ranks[r] and (r in sends.get(c, {}) or r in [p[0] for p in relay.get(c, [])])
 
     def piece(r):
         return T.sp[:, 512 * r:512 * r + 512]
@@ -175,14 +228,7 @@ def rank_program(g, core, T, topo):
         total["ls"] = total.get("ls", 0) + len(bits(m))
 
     def arrives(r):
-        src = ranks[r]
-        if key(src) == key(core):
-            return len(bits(topo.mask(src, core)))
-        gw = gate[(r, key(core))]
-        if gw == core:
-            s = [b for b in sends if core in sends[b].get(r, [])][0]
-            return len(bits(topo.mask(s, core)))
-        return len(bits(topo.mask(gw, core)))
+        return len(bits(topo.mask(come[(core, r)], core)))
 
     near = [b for b in here if topo.die(b) == topo.die(core) and b != core]
     cross = [b for b in here if topo.die(b) != topo.die(core)]
@@ -201,16 +247,9 @@ def rank_program(g, core, T, topo):
         k = once(g.affine_select(T.m1[:], T.m1[:], pat, Op.not_equal, -0.0625, 8, 1))
         wait(g, k)
         km1 = once(g.affine_select(T.m1[:], T.m1[:], pat, Op.not_equal, 0.0625, -120, 1))
-    kip = once(g.iota(T.ip[:], [[0, 8]], 0, 1))
-    kri = once(g.iota(T.ri[:], [[-1, 4], [0, 8], [-4, 16]], 64, 1))
-    kdi = once(g.iota(T.di[:], [[-1, 2], [0, KB], [-2, 8]], 16, 1))
-    kso = once(g.iota(T.so32[:], [[2, 8]], 0, 0))
-    wait(g, k1)
-    k = once(g.affine_select(T.blkf[:], T.blkf[:], [[-16, 8], [0, 16]], Op.is_ge, 0.0, 0, 1))
-    wait(g, k)
-    kblk = once(g.affine_select(T.blkf[:], T.blkf[:], [[16, 8], [0, 16]], Op.is_ge, 0.0, 15, -1))
+        wait(g, "c43", 16)
+        spread(T.vb[:], "b", rank, near + cross)
 
-    if rank is not None:
         wait(V, "c42", 16)
         ka = once(V.tensor_scalar(T.pa[:], T.pt[:], 15, None, Op.bitwise_and))
         kb = once(V.tensor_scalar(T.pb[:], T.pt[:], 4, None, Op.logical_shift_right))
@@ -221,21 +260,32 @@ def rank_program(g, core, T, topo):
         kw = once(V.tensor_tensor(T.pw[:], T.px[:], T.pb[:], Op.add))
         wait(PE, km1)
         wait(PE, kw)
-        PE.matmul(T.wr0[:, 0:256], T.m1[:, 0:128], T.pw[:], True, True)
-        kd = once(PE.matmul(T.wr0[:, 256:512], T.m1[:, 128:256], T.pw[:], True, True))
+        halves = (T.wr0, T.wr1)
+        kd = [once(PE.matmul(halves[u][:, 0:256], T.m1[:, 128 * u:128 * u + 128], T.pw[:], True, True)) for u in range(2)]
         wait(V, kw)
         kw2 = once(V.tensor_scalar(T.w2[:], T.pw[:], 2.0, float(KC), Op.mult, Op.add))
-        wait(V, kd)
-        kh = once(V.tensor_copy(piece(rank), T.wr0[:, 0:512]))
-        wait(V, kh)
-        lo = T.sp[64:128, 512 * rank:512 * rank + 512]
-        kd2 = once(V.tensor_tensor(lo, T.wr0[64:128, 0:512], lo, Op.subtract))
-        wait(g, kh)
-        wait(g, kd2)
+        kh = []
+        for u in range(2):
+            col = slice(512 * rank + 256 * u, 512 * rank + 256 * u + 256)
+            wait(V, kd[u])
+            k = once(V.tensor_copy(T.sp[:, col], halves[u][:, 0:256]))
+            wait(V, k)
+            kh += [k, once(V.tensor_tensor(T.sp[64:128, col], halves[u][64:128, 0:256], T.sp[64:128, col], Op.subtract))]
+        for k in kh:
+            wait(g, k)
         spread(piece(rank), "a", rank, near)
         if own:
             spread(piece(rank), "a", rank, own)
         spread(piece(rank), "a", rank, cross)
+
+    kip = once(g.iota(T.ip[:], [[0, 8]], 0, 1))
+    kri = once(g.iota(T.ri[:], [[-1, 4], [0, 8], [-4, 16]], 64, 1))
+    kdi = once(g.iota(T.di[:], [[-1, 2], [0, KB], [-2, 8]], 16, 1))
+    kso = once(g.iota(T.so32[:], [[2, 8]], 0, 0))
+    wait(g, k1)
+    k = once(g.affine_select(T.blkf[:], T.blkf[:], [[-16, 8], [0, 16]], Op.is_ge, 0.0, 0, 1))
+    wait(g, k)
+    kblk = once(g.affine_select(T.blkf[:], T.blkf[:], [[16, 8], [0, 16]], Op.is_ge, 0.0, 15, -1))
 
     wait(V, kip)
     kq = once(V.tensor_scalar(T.qi[:], T.ip[:], 15, None, Op.bitwise_and))
@@ -273,40 +323,29 @@ def rank_program(g, core, T, topo):
                                             remote_sem=T.sem["wsem"], srcs=[T.w2[:, KW * j:KW * j + KW]], dsts=[T.w1[:]]))
             g.remote_dma_fused(tr, local_sem=T.sem["ls"])
             total["ls"] += n * len(dsts)
-        wait(g, "c43", 16)
-        spread(T.vb[:], "b", rank, near)
         if own:
             spread(T.vb[:], "b", rank, own)
-        spread(T.vb[:], "b", rank, cross)
     else:
         rest = [b for b in here if b != core]
         for sem, src in (("a", stored), ("b", vstored)):
             for r, dsts in sends.get(core, {}).items():
                 wait(g, sem + str(r), arrives(r))
                 spread(src(r), sem, r, dsts)
-            for r in relay.get(core, []):
+            for r, over in relay.get(core, []):
                 wait(g, sem + str(r), arrives(r))
+                if over is not None:
+                    spread(src(r), sem, r, [over])
                 spread(src(r), sem, r, rest)
 
-    def near_rank(r):
-        c = ranks[r]
-        if c == core:
-            return 0
-        if key(c) == key(core):
-            return 1 if topo.die(c) == topo.die(core) else 2
-        if topo.same_plane(c, core):
-            return 3
-        return 4
-
-    order = sorted(range(8), key=near_rank)
+    order = sorted(range(8), key=lambda r: at[(core, r)] + (3 if sends_on(core, r) else 0))
     banks = [T.wr0, T.row0, T.wr1, T.row1]
     wait(PE, krp)
     wait(S, kkc)
     wait(V, kkc)
     for i, r in enumerate(order):
         if r == rank:
-            wait(PE, kh)
-            wait(PE, kd2)
+            for k in kh:
+                wait(PE, k)
         elif sends_on(core, r):
             wait(SY, "a%d" % r, arrives(r))
             total["a%d" % r] = arrives(r)
@@ -354,46 +393,53 @@ def rank_program(g, core, T, topo):
     wait(PE, kblk)
     wait(S, kbc)
     ybase = T.ybuf if rank is not None else T.yb
+    chains = range(NCH)
+    bufs = [[T[x + str(m)] for x in ("wr", "row", "e", "mk", "g")] for m in chains]
     for h in range(HOPS):
         last = h == HOPS - 1
-        for m in range(NCH):
+        for m in chains:
             n = str(m)
-            wr, row, e, mk, G, f, o, off = (T[x + n] for x in ("wr", "row", "e", "mk", "g", "f", "o", "off"))
+            wr, row, e, mk, G = bufs[m]
+            col = slice(KB * m, KB * m + KB)
             if h == 0:
-                w = first[:, KB * m:KB * m + KB]
+                w = first[:, col]
                 for u in range(2):
                     inc(V.tensor_tensor(e[:, u:L:2], w.indirect(T.soff[:, 0:KB // 2]), T.delta[:, H * u:H * u + H], Op.mult), "sE" + n)
-                inc(V.tensor_scalar(f[:], w, 16383.0, 0.5, Op.add, Op.mult), "sO" + n)
+                inc(V.tensor_scalar(T.fi[:, col], w, 16383.0, 0.5, Op.add, Op.mult), "sO")
             else:
                 wait(V, "sW" + n, h)
                 for u in range(2):
                     inc(V.tensor_tensor(e[:, u:L:2], wr[:, 0:H], T.delta[:, H * u:H * u + H], Op.mult), "sE" + n)
-                inc(V.tensor_scalar(f[:], wr[:, 0:H:8], 16383.0, 0.5, Op.add, Op.mult), "sO" + n)
-            wait(V, "sO" + n, 3 * h + 1)
-            inc(V.tensor_scalar(o[:], f[:], 16383, None, Op.bitwise_and), "sO" + n)
-            wait(V, "sO" + n, 3 * h + 2)
-            inc(V.tensor_copy(off[:], o[:]), "sO" + n)
+                inc(V.tensor_scalar(T.fi[:, col], wr[:, 0:H:8], 16383.0, 0.5, Op.add, Op.mult), "sO")
             wait(PE, "sE" + n, 2 * h + 2)
             inc(PE.matmul(row[:, 0:L], T.blkb[:], e[:], True, True), "sR" + n)
             if not last:
                 wait(S, "sR" + n, h + 1)
                 inc(S.activation(mk[:], row[:, 0:L], Act.Sign, bias=T.bcol[:, 0:1]), "sM" + n)
-            wait(V, "sO" + n, 3 * h + 3)
+        wait(V, "sO", (NCH + 2) * h + NCH)
+        inc(V.tensor_scalar(T.oi[:], T.fi[:], 16383, None, Op.bitwise_and), "sO")
+        wait(V, "sO", (NCH + 2) * h + NCH + 1)
+        inc(V.tensor_copy(T.offs[:], T.oi[:]), "sO")
+        if h == 0:
+            for cb in range(4):
+                wait(V, "ev%d" % cb, 8)
+        if last:
+            wait(V, koc)
+            for m in chains:
+                wait(V, "sR%d" % m, h + 1)
+                inc(V.tensor_scalar(bufs[m][3][:], bufs[m][1][:, 0:L], T.ocol[:, 0:1], None, Op.is_equal), "sM%d" % m)
+            wait(V, "vfill", 1024)
+        wait(V, "sO", (NCH + 2) * (h + 1))
+        for m in chains:
+            n = str(m)
+            wr, row, e, mk, G = bufs[m]
+            col = slice(KB * m, KB * m + KB)
+            wait(V, "sM" + n, h + 1)
             if not last:
-                if h == 0 and m == 0:
-                    for cb in range(4):
-                        wait(V, "ev%d" % cb, 8)
-                wait(V, "sM" + n, h + 1)
-                inc(V.tensor_tensor(G[:], T.tab[:, 0:16384].indirect(off[:, 0:KB]), mk[:], Op.mult), "sG" + n)
+                inc(V.tensor_tensor(G[:], T.tab[:, 0:16384].indirect(T.offs[:, col]), mk[:], Op.mult), "sG" + n)
             else:
-                wait(V, koc)
-                wait(V, "sR" + n, h + 1)
-                inc(V.tensor_scalar(mk[:], row[:, 0:L], T.ocol[:, 0:1], None, Op.is_equal), "sM" + n)
-                wait(V, "sM" + n, h + 1)
-                if m == 0:
-                    wait(V, "vfill", 1024)
                 G = T["gv" + n]
-                inc(V.tensor_tensor(G[:], T.vtab[:, 0:16384].indirect(off[:, 0:KB]), mk[:], Op.mult), "sG" + n)
+                inc(V.tensor_tensor(G[:], T.vtab[:, 0:16384].indirect(T.offs[:, col]), mk[:], Op.mult), "sG" + n)
             wait(PE, "sG" + n, h + 1)
             for i in range(L // 128):
                 lhs = G[:, 128 * i:128 * i + 128]
@@ -404,7 +450,7 @@ def rank_program(g, core, T, topo):
                 if i == L // 128 - 1:
                     inc(ins, "sW" + n)
     ky = []
-    for m in range(NCH):
+    for m in chains:
         wait(V, "sW%d" % m, HOPS)
         ky.append(once(V.tensor_copy(ybase[:, KB * m:KB * m + KB], T["wr%d" % m][:, 0:KB])))
 

from concourse.bass import DstId, RemoteDMATransfer
from concourse.mybir import AluOpType as Op, ActivationFunctionType as Act

NCORES = 256
CHIPS_A_HOST = 8
KC = 192 * 32768 - 16383
HOPS = 16
QCORES = CHIPS_A_HOST // 2 * 4
KW = 256 // QCORES
NCH = 2
KB = KW // NCH
L = 16 * KB
H = L // 2

SCRATCH = {
    "tab": ("sbuf", [128, 16384], "float32"),
    "vtab": ("sbuf", [128, 16384], "bfloat16"),
    "sp": ("sbuf", [128, 4096], "float16"),
    "land": ("dram", [1024, 512], "float16"),
    "vland": ("dram", [1024, 256], "bfloat16"),
    "pt": ("sbuf", [128, 256], "int32"),
    "pa": ("sbuf", [128, 256], "int32"),
    "pb": ("sbuf", [128, 256], "int32"),
    "px": ("sbuf", [128, 256], "float32"),
    "pw": ("sbuf", [128, 256], "float32"),
    "w2": ("sbuf", [128, 256], "float32"),
    "vb": ("sbuf", [128, 256], "bfloat16"),
    "m1": ("sbuf", [128, 256], "float32"),
    "ri": ("sbuf", [128, 512], "int32"),
    "rj": ("sbuf", [128, 512], "int32"),
    "rep": ("sbuf", [128, 512], "float16"),
    "kcol": ("sbuf", [128, 8], "float32"),
    "w1": ("sbuf", [128, KW], "float32"),
    "ip": ("sbuf", [128, 8], "int32"),
    "qi": ("sbuf", [128, 8], "int32"),
    "bcol": ("sbuf", [128, 8], "float32"),
    "ocol": ("sbuf", [128, 8], "float32"),
    "di": ("sbuf", [128, L], "int32"),
    "dj": ("sbuf", [128, L], "int32"),
    "delta": ("sbuf", [128, L], "bfloat16"),
    "so32": ("sbuf", [128, 8], "int32"),
    "sb32": ("sbuf", [128, 8], "int32"),
    "sc32": ("sbuf", [128, 8], "int32"),
    "soff": ("sbuf", [128, 8], "uint16"),
    "blkf": ("sbuf", [128, 128], "float32"),
    "blkb": ("sbuf", [128, 128], "bfloat16"),
    "fi": ("sbuf", [128, KW], "int32"),
    "oi": ("sbuf", [128, KW], "int32"),
    "offs": ("sbuf", [128, KW], "uint16"),
    "yb": ("sbuf", [128, KW], "bfloat16"),
    "ybuf": ("sbuf", [128, 256], "bfloat16"),
}
SEMAPHORES = ["sO", "vfill", "ls", "wsem", "ysem", "st"]
for _m in range(8):
    SEMAPHORES += [s + str(_m) for s in ("a", "b", "l")]
for _m in range(4):
    SEMAPHORES += ["pf%d" % _m, "ev%d" % _m]
SEMAPHORES += ["c%d" % i for i in range(44)]
for _m in range(NCH):
    SCRATCH["wr%d" % _m] = ("psum", [128, 512], "float32")
    SCRATCH["row%d" % _m] = ("psum", [128, 512], "float32")
    SCRATCH["e%d" % _m] = ("sbuf", [128, L], "bfloat16")
    SCRATCH["mk%d" % _m] = ("sbuf", [128, L], "bfloat16")
    SCRATCH["g%d" % _m] = ("sbuf", [128, L], "float32")
    SCRATCH["gv%d" % _m] = ("sbuf", [128, L], "bfloat16")
    SEMAPHORES += [s + str(_m) for s in ("sW", "sE", "sR", "sM", "sG")]


def layout(T, topo):
    chips = {}
    for c in range(NCORES):
        chips.setdefault((topo.host(c), topo.chip(c)), []).append(c)
    key = lambda c: (topo.host(c), topo.chip(c))
    mate = {}
    for a in chips:
        for b in chips:
            if topo.mates(chips[a][0], chips[b][0]):
                mate[a] = b
    ranks = list(T.cores)
    homes = set(key(c) for c in ranks)
    work = []
    for h in sorted(set(topo.host(c) for c in ranks)):
        mine = []
        for k in [key(c) for c in ranks if topo.host(c) == h] + [k for k in chips if k[0] == h]:
            for x in (k, mate[k]):
                if x not in mine and len(mine) < CHIPS_A_HOST:
                    mine.append(x)
        work += mine
    free = []
    for x in work:
        if x not in homes and mate[x] not in homes and mate[x] not in free:
            free.append(x)
    entry = {}
    for r, c in enumerate(ranks):
        for x in work:
            if x == key(c):
                continue
            if x == mate[key(c)]:
                entry[(r, x)] = x
                continue
            near = x if topo.same_plane(c, chips[x][0]) else mate[x]
            pair = x if x in free else mate[x]
            over = pair in free and (free.index(pair) + topo.host(c)) % 2 == 0
            entry[(r, x)] = mate[near] if over else near
    sends, relay, gate, load = {}, {}, {}, {}
    for x in work:
        for first in (True, False):
            for r, c in enumerate(ranks):
                if x == key(c) or (entry[(r, x)] == x) != first:
                    continue
                can = [b for b in chips[x] if topo.die(b) == topo.die(c) and b not in ranks]
                owns = [b for b in can if topo.may_write(b, chips[mate[x]][0])]
                if first and x != mate[key(c)]:
                    can = owns
                elif first:
                    can = [b for b in can if b not in owns]
                b = min(can, key=lambda b: load.get(b, 0))
                gate[(r, x)] = b
                load[b] = load.get(b, 0) + 1
    qcores = []
    for r, c in enumerate(ranks):
        d = topo.die(c)
        q = [b for b in chips[key(c)] if topo.die(b) == d and b != c]
        for x in work:
            if x[0] == topo.host(c) and topo.same_plane(c, chips[x][0]):
                q += [b for b in chips[x] if topo.die(b) == d]
        qcores.append([c] + q)
        team = [b for b in chips[key(c)] if topo.die(b) == d]
        far = [x for x in work if x != key(c) and entry[(r, x)] == x]
        far.sort(key=lambda x: (sum(topo.may_write(b, gate[(r, x)]) for b in team), x == mate[key(c)]))
        load[c] = 1
        for x in far:
            b = min([b for b in team if topo.may_write(b, gate[(r, x)])], key=lambda b: load.get(b, 0))
            load[b] = load.get(b, 0) + 1
            sends.setdefault(b, {}).setdefault(r, []).append(gate[(r, x)])
    come, at = {}, {}
    for r, c in enumerate(ranks):
        at[(c, r)] = 0
        for b in chips[key(c)]:
            if b != c:
                come[(b, r)] = c
                at[(b, r)] = 4 if topo.die(b) == topo.die(c) else 8
    for r, c in enumerate(ranks):
        for b in sends:
            for i, y in enumerate(sends[b].get(r, [])):
                come[(y, r)] = b
                at[(y, r)] = at[(b, r)] + (6 if b == c else 4) + i
    for first in (True, False):
        for x in work:
            ways = sorted((at.get((gate[(r, x)], r), 0), r) for r, c in enumerate(ranks)
                          if x != key(c) and (entry[(r, x)] == x) == first)
            for _, r in ways:
                c, y = ranks[r], gate[(r, x)]
                if not first:
                    o = gate[(r, mate[x])]
                    come[(y, r)] = o
                    at[(y, r)] = at[(o, r)] + 4
                n = gate[(r, mate[x])] if first and x != mate[key(c)] else None
                relay.setdefault(y, []).append((r, n))
                for b in chips[x]:
                    if b != y:
                        come[(b, r)] = y
                        at[(b, r)] = at[(y, r)] + (7 if n is not None else 6)
    for c in relay:
        relay[c].sort(key=lambda p: at[(c, p[0])])
    return chips, key, work, qcores, sends, relay, come, at


def bits(m):
    return [1 << i for i in range(16) if m >> i & 1]


_cache = {}


def rank_program(g, core, T, topo):
    if "lay" not in _cache:
        _cache["lay"] = layout(T, topo)
    chips, key, work, qcores, sends, relay, come, at = _cache["lay"]
    if key(core) not in work:
        return
    ranks = list(T.cores)
    rank = T.rank_of(core)
    here = chips[key(core)]
    V, S, PE, SY = g.vector, g.scalar, g.tensor, g.sync
    owner = [r for r in range(8) if core in qcores[r]][0]
    t = qcores[owner].index(core)
    total = {}
    nc = [0]

    def inc(ins, name, n=1):
        ins.then_inc(T.sem[name], n)
        total[name] = total.get(name, 0) + n

    def once(ins):
        name = "c%d" % nc[0]
        nc[0] += 1
        inc(ins, name)
        return name

    def wait(q, name, n=1):
        q.wait_ge(T.sem[name], n)

    def dst(d):
        rid, pid = topo.addr(d, core)
        return DstId(rid=rid, pnc=pid)

    def sends_on(c, r):
        return c != ranks[r] and (r in sends.get(c, {}) or r in [p[0] for p in relay.get(c, [])])

    def piece(r):
        return T.sp[:, 512 * r:512 * r + 512]

    def stored(r):
        return T.land[128 * r:128 * r + 128, :]

    def vstored(r):
        return T.vland[128 * r:128 * r + 128, :]

    def spread(src, sem, r, dsts):
        m = topo.mask(core, dsts[0])
        if sem == "a":
            out = [stored(r) if sends_on(d, r) else piece(r) for d in dsts]
        else:
            out = [vstored(r) for d in dsts]
        g.remote_dma_fused([RemoteDMATransfer(dst_ids=[dst(d) for d in dsts], dma_engine_mask=m, remote_sem=T.sem[sem + str(r)],
                                              srcs=[src], dsts=out)], local_sem=T.sem["ls"])
        total["ls"] = total.get("ls", 0) + len(bits(m))

    def arrives(r):
        return len(bits(topo.mask(come[(core, r)], core)))

    near = [b for b in here if topo.die(b) == topo.die(core) and b != core]
    cross = [b for b in here if topo.die(b) != topo.die(core)]
    own = sends.get(core, {}).get(rank, [])

    k1 = once(V.memset(T.blkf[:], 1.0))
    if rank is not None:
        SY.dma_start(T.pt[:], T.par[:]).then_inc(T.sem["c42"], 16)
        S.dma_start(T.vb[:], T.val[:]).then_inc(T.sem["c43"], 16)
        total["c42"] = total["c43"] = 16
        k = once(V.memset(T.m1[:], 0.0))
        wait(g, k)
        pat = [[-1, 2], [0, 2], [-2, 64]]
        k = once(g.affine_select(T.m1[:], T.m1[:], pat, Op.not_equal, 0.0625, 0, 1))
        wait(g, k)
        k = once(g.affine_select(T.m1[:], T.m1[:], pat, Op.not_equal, -0.0625, 8, 1))
        wait(g, k)
        km1 = once(g.affine_select(T.m1[:], T.m1[:], pat, Op.not_equal, 0.0625, -120, 1))
        wait(g, "c43", 16)
        spread(T.vb[:], "b", rank, near + cross)

        wait(V, "c42", 16)
        ka = once(V.tensor_scalar(T.pa[:], T.pt[:], 15, None, Op.bitwise_and))
        kb = once(V.tensor_scalar(T.pb[:], T.pt[:], 4, None, Op.logical_shift_right))
        wait(V, ka)
        kx = once(V.tensor_scalar(T.px[:], T.pa[:], 16384.0, None, Op.mult))
        wait(V, kb)
        wait(V, kx)
        kw = once(V.tensor_tensor(T.pw[:], T.px[:], T.pb[:], Op.add))
        wait(PE, km1)
        wait(PE, kw)
        halves = (T.wr0, T.wr1)
        kd = [once(PE.matmul(halves[u][:, 0:256], T.m1[:, 128 * u:128 * u + 128], T.pw[:], True, True)) for u in range(2)]
        wait(V, kw)
        kw2 = once(V.tensor_scalar(T.w2[:], T.pw[:], 2.0, float(KC), Op.mult, Op.add))
        kh = []
        for u in range(2):
            col = slice(512 * rank + 256 * u, 512 * rank + 256 * u + 256)
            wait(V, kd[u])
            k = once(V.tensor_copy(T.sp[:, col], halves[u][:, 0:256]))
            wait(V, k)
            kh += [k, once(V.tensor_tensor(T.sp[64:128, col], halves[u][64:128, 0:256], T.sp[64:128, col], Op.subtract))]
        for k in kh:
            wait(g, k)
        spread(piece(rank), "a", rank, near)
        if own:
            spread(piece(rank), "a", rank, own)
        spread(piece(rank), "a", rank, cross)

    kip = once(g.iota(T.ip[:], [[0, 8]], 0, 1))
    kri = once(g.iota(T.ri[:], [[-1, 4], [0, 8], [-4, 16]], 64, 1))
    kdi = once(g.iota(T.di[:], [[-1, 2], [0, KB], [-2, 8]], 16, 1))
    kso = once(g.iota(T.so32[:], [[2, 8]], 0, 0))
    wait(g, k1)
    k = once(g.affine_select(T.blkf[:], T.blkf[:], [[-16, 8], [0, 16]], Op.is_ge, 0.0, 0, 1))
    wait(g, k)
    kblk = once(g.affine_select(T.blkf[:], T.blkf[:], [[16, 8], [0, 16]], Op.is_ge, 0.0, 15, -1))

    wait(V, kip)
    kq = once(V.tensor_scalar(T.qi[:], T.ip[:], 15, None, Op.bitwise_and))
    ks1 = once(V.tensor_scalar(T.sb32[:], T.ip[:], 3, 1, Op.logical_shift_right, Op.bitwise_and))
    wait(V, kri)
    krj = once(V.tensor_scalar(T.rj[:], T.ri[:], 63, None, Op.bitwise_and))
    wait(V, kq)
    kkc = once(V.tensor_scalar(T.kcol[:], T.qi[:], 0.0, float(KC), Op.is_equal, Op.mult))
    kbc = once(V.tensor_scalar(T.bcol[:], T.qi[:], -32768.0, -191.5 * 32768, Op.mult, Op.add))
    koc = once(V.tensor_scalar(T.ocol[:], T.qi[:], 32768.0, 192.0 * 32768, Op.mult, Op.add))
    wait(V, krj)
    krp = once(V.tensor_scalar(T.rep[:], T.rj[:], 0.0, 16.0, Op.is_equal, Op.mult))
    wait(V, kdi)
    kdj = once(V.tensor_scalar(T.dj[:], T.di[:], 15, None, Op.bitwise_and))
    wait(V, kso)
    wait(V, ks1)
    ks2 = once(V.tensor_tensor(T.sc32[:], T.so32[:], T.sb32[:], Op.add))
    wait(V, kdj)
    kdl = once(V.tensor_scalar(T.delta[:], T.dj[:], 0.0, None, Op.is_equal))
    wait(V, ks2)
    ksf = once(V.tensor_copy(T.soff[:], T.sc32[:]))
    wait(V, kblk)
    kbb = once(V.tensor_copy(T.blkb[:], T.blkf[:]))

    if rank is not None:
        wait(g, kw2)
        qn = [b for b in qcores[rank] if key(b) == key(core) and b != core]
        far = [b for b in qcores[rank] if key(b) != key(core)]
        calls = [(qn, 4)] + [(far[i:i + 4], 2) for i in range(0, len(far), 4)]
        for dsts, n in calls:
            tr = []
            for i, d in enumerate(dsts):
                j = qcores[rank].index(d)
                tr.append(RemoteDMATransfer(dst_ids=[dst(d)], dma_engine_mask=sum(bits(topo.mask(core, d))[n * i:n * i + n]),
                                            remote_sem=T.sem["wsem"], srcs=[T.w2[:, KW * j:KW * j + KW]], dsts=[T.w1[:]]))
            g.remote_dma_fused(tr, local_sem=T.sem["ls"])
            total["ls"] += n * len(dsts)
        if own:
            spread(T.vb[:], "b", rank, own)
    else:
        rest = [b for b in here if b != core]
        for sem, src in (("a", stored), ("b", vstored)):
            for r, dsts in sends.get(core, {}).items():
                wait(g, sem + str(r), arrives(r))
                spread(src(r), sem, r, dsts)
            for r, over in relay.get(core, []):
                wait(g, sem + str(r), arrives(r))
                if over is not None:
                    spread(src(r), sem, r, [over])
                spread(src(r), sem, r, rest)

    order = sorted(range(8), key=lambda r: at[(core, r)] + (3 if sends_on(core, r) else 0))
    banks = [T.wr0, T.row0, T.wr1, T.row1]
    wait(PE, krp)
    wait(S, kkc)
    wait(V, kkc)
    for i, r in enumerate(order):
        if r == rank:
            for k in kh:
                wait(PE, k)
        elif sends_on(core, r):
            wait(SY, "a%d" % r, arrives(r))
            total["a%d" % r] = arrives(r)
            inc(SY.dma_start(piece(r), stored(r)), "l%d" % r, 16)
            wait(PE, "l%d" % r, 16)
        else:
            wait(PE, "a%d" % r, arrives(r))
            total["a%d" % r] = arrives(r)
        for cb in range(4):
            n = str(cb)
            if i:
                wait(PE, "ev" + n, i)
            inc(PE.matmul(banks[cb][:, 0:512], T.rep[:, 128 * cb:128 * cb + 128], piece(r), True, True), "pf" + n)
            out = T.tab[:, 2048 * r + 512 * cb:2048 * r + 512 * cb + 512]
            if cb % 2 == 0:
                wait(V, "pf" + n, i + 1)
                inc(V.tensor_scalar(out, banks[cb][:, 0:512], T.kcol[:, 0:1], None, Op.add), "ev" + n)
            else:
                wait(S, "pf" + n, i + 1)
                inc(S.activation(out, banks[cb][:, 0:512], Act.Identity, bias=T.kcol[:, 0:1]), "ev" + n)
    for cb in range(4):
        wait(PE, "ev%d" % cb, 8)
    for r in order:
        if r == rank:
            wait(SY, "c43", 16)
            src = T.vb[:]
        else:
            wait(SY, "b%d" % r, arrives(r))
            total["b%d" % r] = arrives(r)
            src = vstored(r)
        for i in range(8):
            inc(SY.dma_start(T.vtab[16 * i:16 * i + 16, 2048 * r:2048 * r + 2048], src), "vfill", 16)

    if rank is None:
        nw = 4 if key(core) == key(ranks[owner]) else 2
        total["wsem"] = nw
        wait(V, "wsem", nw)
        first = T.w1
    else:
        wait(V, kw2)
        first = T.w2
    wait(V, ksf)
    wait(V, kdl)
    wait(PE, kbb)
    wait(PE, kblk)
    wait(S, kbc)
    ybase = T.ybuf if rank is not None else T.yb
    chains = range(NCH)
    bufs = [[T[x + str(m)] for x in ("wr", "row", "e", "mk", "g")] for m in chains]
    for h in range(HOPS):
        last = h == HOPS - 1
        for m in chains:
            n = str(m)
            wr, row, e, mk, G = bufs[m]
            col = slice(KB * m, KB * m + KB)
            if h == 0:
                w = first[:, col]
                for u in range(2):
                    inc(V.tensor_tensor(e[:, u:L:2], w.indirect(T.soff[:, 0:KB // 2]), T.delta[:, H * u:H * u + H], Op.mult), "sE" + n)
                inc(V.tensor_scalar(T.fi[:, col], w, 16383.0, 0.5, Op.add, Op.mult), "sO")
            else:
                wait(V, "sW" + n, h)
                for u in range(2):
                    inc(V.tensor_tensor(e[:, u:L:2], wr[:, 0:H], T.delta[:, H * u:H * u + H], Op.mult), "sE" + n)
                inc(V.tensor_scalar(T.fi[:, col], wr[:, 0:H:8], 16383.0, 0.5, Op.add, Op.mult), "sO")
            wait(PE, "sE" + n, 2 * h + 2)
            inc(PE.matmul(row[:, 0:L], T.blkb[:], e[:], True, True), "sR" + n)
            if not last:
                wait(S, "sR" + n, h + 1)
                inc(S.activation(mk[:], row[:, 0:L], Act.Sign, bias=T.bcol[:, 0:1]), "sM" + n)
        wait(V, "sO", (NCH + 2) * h + NCH)
        inc(V.tensor_scalar(T.oi[:], T.fi[:], 16383, None, Op.bitwise_and), "sO")
        wait(V, "sO", (NCH + 2) * h + NCH + 1)
        inc(V.tensor_copy(T.offs[:], T.oi[:]), "sO")
        if h == 0:
            for cb in range(4):
                wait(V, "ev%d" % cb, 8)
        if last:
            wait(V, koc)
            for m in chains:
                wait(V, "sR%d" % m, h + 1)
                inc(V.tensor_scalar(bufs[m][3][:], bufs[m][1][:, 0:L], T.ocol[:, 0:1], None, Op.is_equal), "sM%d" % m)
            wait(V, "vfill", 1024)
        wait(V, "sO", (NCH + 2) * (h + 1))
        for m in chains:
            n = str(m)
            wr, row, e, mk, G = bufs[m]
            col = slice(KB * m, KB * m + KB)
            wait(V, "sM" + n, h + 1)
            if not last:
                inc(V.tensor_tensor(G[:], T.tab[:, 0:16384].indirect(T.offs[:, col]), mk[:], Op.mult), "sG" + n)
            else:
                G = T["gv" + n]
                inc(V.tensor_tensor(G[:], T.vtab[:, 0:16384].indirect(T.offs[:, col]), mk[:], Op.mult), "sG" + n)
            wait(PE, "sG" + n, h + 1)
            for i in range(L // 128):
                lhs = G[:, 128 * i:128 * i + 128]
                if not last:
                    ins = PE.matmul(wr[:, 64 * i:64 * i + 64], lhs, T.blkf[:, 0:128:2], True, True)
                else:
                    ins = PE.matmul(wr[:, 8 * i:8 * i + 8], lhs, T.blkb[:, 0:128:16], True, True)
                if i == L // 128 - 1:
                    inc(ins, "sW" + n)
    ky = []
    for m in chains:
        wait(V, "sW%d" % m, HOPS)
        ky.append(once(V.tensor_copy(ybase[:, KB * m:KB * m + KB], T["wr%d" % m][:, 0:KB])))

    if rank is None:
        for k in ky:
            wait(g, k)
        d = ranks[owner]
        m = sum(bits(topo.mask(core, d))[:8])
        g.remote_dma(T.ybuf[:, KW * t:KW * t + KW], T.yb[:], T.sem["ysem"], T.sem["ls"], topo.addr(d, core)[1], topo.addr(d, core)[0], m)
        total["ls"] = total.get("ls", 0) + 8
    else:
        total["ysem"] = 8 * (QCORES - 1)
        for k in ky:
            wait(SY, k)
        wait(SY, "ysem", total["ysem"])
        inc(SY.dma_start(T.y[:], T.ybuf[:]), "st", 16)
    for name, n in total.items():
        wait(g, name, n)
